import numpy as np, ml_dtypes
CORES = [24,26,29,31,48,50,53,55]
N = 8
T, M = 8192, 2048
def entries(a): return a.T.reshape(-1)
def pack(v, P): return np.ascontiguousarray(np.asarray(v, np.int32).reshape(-1, P).T)
def lists(rng, how):
    I = rng.integers(0, T, (N, M))
    if how == "alike": I[:] = rng.integers(0, T, (N, 1))
    if how == "distinct": I = np.stack([rng.permutation(T)[:M] for r in range(N)])
    if how == "sorted": I = np.sort(I, axis=1)
    if how == "edge": I = np.where(rng.random((N, M)) < 0.5, 0, T - 1)
    return {"idx": np.stack([pack(I[r], 16) for r in range(N)])}
def setup_inputs(rng):
    return dict({"x": rng.standard_normal((N, 128, T), dtype=np.float32).astype(ml_dtypes.bfloat16)}, **lists(rng, "uniform"))
def setup_inputs_alike(rng):
    d = setup_inputs(rng); d.update(lists(rng, "alike"))
    for k in ("x",): d[k] = (d[k].astype(np.float32) * 1024.0).astype(d[k].dtype)
    return d
def setup_inputs_distinct(rng):
    d = setup_inputs(rng); d.update(lists(rng, "distinct"))
    for k in ("x",): d[k] = (d[k].astype(np.float32) * (1 / 1024.0)).astype(d[k].dtype)
    return d
def setup_inputs_edge(rng):
    d = setup_inputs(rng); d.update(lists(rng, "edge"))
    return d
def setup_inputs_sorted(rng):
    d = setup_inputs(rng); d.update(lists(rng, "sorted"))
    return d
def check_inputs(x):
    bad = []
    if x["idx"].min() < 0 or x["idx"].max() >= T: bad.append("idx out of range")
    return bad
def reference(x, idx):
    s = sum(x[r].astype(np.float64)[:, entries(idx[r])] for r in range(N)).astype(ml_dtypes.bfloat16)
    return {"y": np.broadcast_to(s, (N, 128, M))}

@@ -1,0 +1,242 @@
+from concourse.bass import DstId, RemoteDMATransfer
+from concourse.mybir import AluOpType, ActivationFunctionType
+
+SIM_CORES = 64
+NCOL = 8192
+M = 2048
+C = 2
+W = M // C
+WB = 0
+WA = W // 2 - WB
+SLOT = M // 2
+NB = (WA + 511) // 512
+BW = WA // NB
+
+SCRATCH = {
+    "xs": ("sbuf", [128, NCOL], "bfloat16"),
+    "idx32": ("sbuf", [128, 128], "int32"),
+    "idxf": ("sbuf", [128, 128], "float32"),
+    "onesf": ("sbuf", [128, 128], "float32"),
+    "rep": ("sbuf", [128, 128], "float32"),
+    "onesb": ("sbuf", [128, 128], "bfloat16"),
+    "ident": ("sbuf", [128, 128], "bfloat16"),
+    "offs": ("sbuf", [128, 128], "uint16"),
+    "gat": ("sbuf", [128, M], "bfloat16"),
+    "land1": ("sbuf", [128, 4 * SLOT], "bfloat16"),
+    "land2": ("sbuf", [128, SLOT], "bfloat16"),
+    "res": ("sbuf", [128, M], "bfloat16"),
+    "psoff": ("psum", [128, 128], "float32"),
+    "ps": ("psum", [128, 512 * C * NB], "float32"),
+}
+SEMAPHORES = (["six", "sx", "sone", "srep", "sid", "sf", "spo", "soff", "sent", "st0", "st1"]
+              + ["gat%d" % c for c in range(C)] + ["a1_%d" % c for c in range(C)] + ["a2_%d" % c for c in range(C)]
+              + ["a3_%d_%d" % (c, p) for c in range(C) for p in range(2)]
+              + ["mm%d" % c for c in range(C)] + ["own%d" % c for c in range(C)])
+
+
+def _bits(mask):
+    return [e for e in range(mask.bit_length()) if (mask >> e) & 1]
+
+
+def _mask(engs):
+    m = 0
+    for e in engs:
+        m |= 1 << e
+    return m
+
+
+def _layout(T, topo):
+    ranks = list(T.cores)
+    lay = {}
+    for ch in sorted({topo.chip(c) for c in ranks}):
+        mine = [c for c in ranks if topo.chip(c) == ch]
+        far = [c for c in ranks if topo.chip(c) != ch]
+        here = [c for c in range(SIM_CORES) if topo.chip(c) == ch]
+        owners = []
+        for part, d in enumerate(sorted({topo.die(c) for c in mine})):
+            port = [c for c in here if topo.die(c) == d and all(topo.may_write(c, f) for f in far)]
+            picks = [([c for c in port if c in mine][0], WA)]
+            if WB:
+                picks.append(([c for c in port if c not in mine][0], WB))
+            off = part * (W // 2)
+            for c, w in picks:
+                owners.append({"core": c, "die": d, "part": part, "w": w, "off": off})
+                off += w
+        lay[ch] = (mine, owners)
+    return lay
+
+
+def _s1_calls(topo, sender, owners):
+    calls = []
+    for w in sorted({o["w"] for o in owners}):
+        tg = [i for i, o in enumerate(owners) if o["w"] == w and o["core"] != sender]
+        if not tg:
+            continue
+        m = topo.mask(sender, owners[tg[0]]["core"])
+        for i in tg:
+            m &= topo.mask(sender, owners[i]["core"])
+        engs = _bits(m)
+        near = [i for i in tg if owners[i]["die"] == topo.die(sender)]
+        far = [i for i in tg if owners[i]["die"] != topo.die(sender)]
+        pools = [(near, engs[0::2]), (far, engs[1::2])] if near and far else [(near or far, engs)]
+        call = []
+        for grp, pool in pools:
+            n = len(pool) // len(grp)
+            for k, i in enumerate(grp):
+                call.append((i, pool[k * n:(k + 1) * n]))
+        calls.append(call)
+    return calls
+
+
+def _dst(topo, c):
+    rid, pid, _ = topo.addr(c)
+    return DstId(rid=rid, pnc=pid)
+
+
+def rank_program(g, core, T, topo):
+    lay = _layout(T, topo)
+    ch = topo.chip(core)
+    if ch not in lay:
+        return
+    mine, owners = lay[ch]
+    peers = [lay[k] for k in lay if k != ch][0][1]
+    me = [i for i, o in enumerate(owners) if o["core"] == core]
+    me = me[0] if me else None
+    is_rank = core in mine
+    if not is_rank and me is None:
+        return
+    S = T.sem
+    v, sc, sy, te = g.vector, g.scalar, g.sync, g.tensor
+    sent = 0
+
+    if is_rank:
+        sc.dma_start(T.idx32[0:16, :], T.idx[:, :]).then_inc(S.six, 16)
+        sy.dma_start(T.xs[:, :], T.x[:, :]).then_inc(S.sx, 16)
+        v.memset(T.onesf[0:16, :], 1.0).then_inc(S.sone, 1)
+        n1 = 1
+        if me is not None:
+            v.memset(T.onesb[:, :], 1.0).then_inc(S.sone, 1)
+            n1 = 2
+        g.wait_ge(S.sone, n1)
+        g.affine_select(T.rep[0:16, :], T.onesf[0:16, :], [[0, 8], [-1, 16]], AluOpType.is_equal, 0.0, 0, 1).then_inc(S.srep, 1)
+        if me is not None:
+            g.affine_select(T.ident[:, :], T.onesb[:, :], [[-1, 128]], AluOpType.is_equal, 0.0, 0, 1).then_inc(S.sid, 1)
+        v.wait_ge(S.six, 16)
+        v.tensor_copy(T.idxf[0:16, :], T.idx32[0:16, :]).then_inc(S.sf, 1)
+        te.wait_ge(S.sf, 1)
+        te.wait_ge(S.srep, 1)
+        te.matmul(T.psoff[:, :], T.rep[0:16, :], T.idxf[0:16, :], True, True).then_inc(S.spo, 1)
+        v.wait_ge(S.spo, 1)
+        v.tensor_copy(T.offs[:, :], T.psoff[:, :]).then_inc(S.soff, 1)
+        for q in (v, sc):
+            q.wait_ge(S.soff, 1)
+            q.wait_ge(S.sx, 16)
+        h = W // 2
+        for c in range(C):
+            a = c * W
+            v.tensor_copy(T.gat[:, a:a + h],
+                          T.xs[:, 0:NCOL].indirect(T.offs[:, a // 16:(a + h) // 16])).then_inc(S["gat%d" % c], 1)
+            a += h
+            sc.activation(T.gat[:, a:a + h], T.xs[:, 0:NCOL].indirect(T.offs[:, a // 16:(a + h) // 16]),
+                          ActivationFunctionType.Copy).then_inc(S["gat%d" % c], 1)
+        pos = mine.index(core)
+        calls = _s1_calls(topo, core, owners)
+        for c in range(C):
+            g.wait_ge(S["gat%d" % c], 2)
+            for call in calls:
+                trs = []
+                for i, engs in call:
+                    o = owners[i]
+                    y0 = c * W + o["off"]
+                    l0 = pos * SLOT + c * o["w"]
+                    trs.append(RemoteDMATransfer(dst_ids=[_dst(topo, o["core"])], dma_engine_mask=_mask(engs),
+                                                 remote_sem=S["a1_%d" % c], src=T.gat[:, y0:y0 + o["w"]],
+                                                 dst=T.land1[:, l0:l0 + o["w"]]))
+                    sent += len(engs)
+                g.remote_dma_fused(trs, local_sem=S.sent)
+
+    if me is not None:
+        o = owners[me]
+        w = o["w"]
+        peer = peers[me]["core"]
+        exp1 = 0
+        for r in mine:
+            if r != core:
+                for call in _s1_calls(topo, r, owners):
+                    exp1 += sum(len(engs) for i, engs in call if i == me)
+        exp2 = len(_bits(topo.mask(peer, core)))
+
+        def pieces(c, lo, n):
+            out = []
+            for s, r in enumerate(mine):
+                if r == core:
+                    out.append(T.gat[:, c * W + o["off"] + lo:c * W + o["off"] + lo + n])
+                else:
+                    out.append(T.land1[:, s * SLOT + c * w + lo:s * SLOT + c * w + lo + n])
+            return out
+
+        e2 = _bits(topo.mask(core, peer))
+        for c in range(C):
+            g.wait_ge(S["a1_%d" % c], exp1)
+            g.remote_dma_fused([RemoteDMATransfer(dst_ids=[_dst(topo, peer)], dma_engine_mask=_mask(e2),
+                                                  remote_sem=S["a2_%d" % c], srcs=pieces(c, 0, w),
+                                                  dsts=[T.land2[:, c * w:(c + 1) * w]], alu_op=1)], local_sem=S.sent)
+            sent += len(e2)
+        dests = [r for r in mine if r != core]
+        m3 = topo.mask(core, dests[0])
+        for r in dests:
+            m3 &= topo.mask(core, r)
+        e3 = _bits(m3)
+        for c in range(C):
+            g.wait_ge(S["a2_%d" % c], exp2)
+            y0 = c * W + o["off"]
+            g.remote_dma_fused([RemoteDMATransfer(dst_ids=[_dst(topo, r) for r in dests], dma_engine_mask=_mask(e3),
+                                                  remote_sem=S["a3_%d_%d" % (c, o["part"])],
+                                                  srcs=pieces(c, 0, w) + [T.land2[:, c * w:(c + 1) * w]],
+                                                  dsts=[T.res[:, y0:y0 + w] for r in dests], alu_op=1)],
+                               local_sem=S.sent)
+            sent += len(e3)
+        if is_rank:
+            te.wait_ge(S.sid, 1)
+            for c in range(C):
+                te.wait_ge(S["gat%d" % c], 2)
+                te.wait_ge(S["a1_%d" % c], exp1)
+                for b in range(NB):
+                    p0 = (c * NB + b) * 512
+                    for k, src in enumerate(pieces(c, b * BW, BW)):
+                        te.matmul(T.ps[:, p0:p0 + BW], T.ident[:, :], src, k == 0, False)
+            for c in range(C):
+                te.wait_ge(S["a2_%d" % c], exp2)
+                for b in range(NB):
+                    p0 = (c * NB + b) * 512
+                    te.matmul(T.ps[:, p0:p0 + BW], T.ident[:, :], T.land2[:, c * w + b * BW:c * w + (b + 1) * BW],
+                              False, True).then_inc(S["mm%d" % c], 1)
+            for c in range(C):
+                v.wait_ge(S["mm%d" % c], NB)
+                for b in range(NB):
+                    p0 = (c * NB + b) * 512
+                    y0 = c * W + o["off"] + b * BW
+                    v.tensor_copy(T.res[:, y0:y0 + BW], T.ps[:, p0:p0 + BW]).then_inc(S["own%d" % c], 1)
+
+    if is_rank:
+        h = W // 2
+        for c in range(C):
+            for part, q in enumerate((sy, sc)):
+                exp3 = 0
+                for i, o in enumerate(owners):
+                    if o["part"] == part and o["core"] != core:
+                        ds = [r for r in mine if r != o["core"]]
+                        m = topo.mask(o["core"], ds[0])
+                        for r in ds:
+                            m &= topo.mask(o["core"], r)
+                        exp3 += len(_bits(m))
+                if exp3:
+                    q.wait_ge(S["a3_%d_%d" % (c, part)], exp3)
+                if me is not None and owners[me]["part"] == part:
+                    q.wait_ge(S["own%d" % c], NB)
+                a = c * W + part * h
+                q.dma_start(T.y[:, a:a + h], T.res[:, a:a + h]).then_inc(S["st%d" % part], 16)
+        sy.wait_ge(S.st0, 16 * C)
+        sc.wait_ge(S.st1, 16 * C)
+
+    g.wait_ge(S.sent, sent)

@@ -4,13 +4,10 @@ from concourse.mybir import AluOpType, ActivationFunctionType
 SIM_CORES = 64
 NCOL = 8192
 M = 2048
-C = 2
+C = 4
 W = M // C
-WB = 0
-WA = W // 2 - WB
-SLOT = M // 2
-NB = (WA + 511) // 512
-BW = WA // NB
+H = W // 2
+SLOT = (C // 2) * H
 
 SCRATCH = {
     "xs": ("sbuf", [128, NCOL], "bfloat16"),
@@ -18,20 +15,21 @@ SCRATCH = {
     "idxf": ("sbuf", [128, 128], "float32"),
     "onesf": ("sbuf", [128, 128], "float32"),
     "rep": ("sbuf", [128, 128], "float32"),
-    "onesb": ("sbuf", [128, 128], "bfloat16"),
-    "ident": ("sbuf", [128, 128], "bfloat16"),
     "offs": ("sbuf", [128, 128], "uint16"),
     "gat": ("sbuf", [128, M], "bfloat16"),
     "land1": ("sbuf", [128, 4 * SLOT], "bfloat16"),
+    "landp": ("sbuf", [128, SLOT], "bfloat16"),
     "land2": ("sbuf", [128, SLOT], "bfloat16"),
     "res": ("sbuf", [128, M], "bfloat16"),
     "psoff": ("psum", [128, 128], "float32"),
-    "ps": ("psum", [128, 512 * C * NB], "float32"),
 }
-SEMAPHORES = (["six", "sx", "sone", "srep", "sid", "sf", "spo", "soff", "sent", "st0", "st1"]
+SEMAPHORES = (["six", "sx", "sone", "srep", "sf", "spo", "soff", "sent", "st0", "st1"]
               + ["gat%d" % c for c in range(C)] + ["a1_%d" % c for c in range(C)] + ["a2_%d" % c for c in range(C)]
-              + ["a3_%d_%d" % (c, p) for c in range(C) for p in range(2)]
-              + ["mm%d" % c for c in range(C)] + ["own%d" % c for c in range(C)])
+              + ["a3_%d_%d" % (c, p) for c in range(C) for p in range(2)])
+
+
+def _kind(c):
+    return (c + 1) % 2
 
 
 def _bits(mask):
@@ -45,6 +43,13 @@ def _mask(engs):
     return m
 
 
+def _common(topo, src, dsts):
+    m = topo.mask(src, dsts[0])
+    for d in dsts:
+        m &= topo.mask(src, d)
+    return _bits(m)
+
+
 def _layout(T, topo):
     ranks = list(T.cores)
     lay = {}
@@ -52,40 +57,42 @@ def _layout(T, topo):
         mine = [c for c in ranks if topo.chip(c) == ch]
         far = [c for c in ranks if topo.chip(c) != ch]
         here = [c for c in range(SIM_CORES) if topo.chip(c) == ch]
-        owners = []
-        for part, d in enumerate(sorted({topo.die(c) for c in mine})):
-            port = [c for c in here if topo.die(c) == d and all(topo.may_write(c, f) for f in far)]
-            picks = [([c for c in port if c in mine][0], WA)]
-            if WB:
-                picks.append(([c for c in port if c not in mine][0], WB))
-            off = part * (W // 2)
-            for c, w in picks:
-                owners.append({"core": c, "die": d, "part": part, "w": w, "off": off})
-                off += w
-        lay[ch] = (mine, owners)
+        own = [[], []]
+        for d in sorted({topo.die(c) for c in mine}):
+            on_die = [c for c in here if topo.die(c) == d]
+            port = [c for c in on_die if all(topo.may_write(c, f) for f in far)]
+            rk = [c for c in port if c in mine][0]
+            hp = [c for c in port if c not in mine][0]
+            hn = [c for c in on_die if c not in mine and c not in port][0]
+            own[0].append({"sum": rk, "fin": hn, "die": d})
+            own[1].append({"sum": hp, "fin": hp, "die": d})
+        lay[ch] = (mine, own)
     return lay
 
 
-def _s1_calls(topo, sender, owners):
-    calls = []
-    for w in sorted({o["w"] for o in owners}):
-        tg = [i for i, o in enumerate(owners) if o["w"] == w and o["core"] != sender]
-        if not tg:
-            continue
-        m = topo.mask(sender, owners[tg[0]]["core"])
-        for i in tg:
-            m &= topo.mask(sender, owners[i]["core"])
-        engs = _bits(m)
-        near = [i for i in tg if owners[i]["die"] == topo.die(sender)]
-        far = [i for i in tg if owners[i]["die"] != topo.die(sender)]
-        pools = [(near, engs[0::2]), (far, engs[1::2])] if near and far else [(near or far, engs)]
-        call = []
-        for grp, pool in pools:
-            n = len(pool) // len(grp)
-            for k, i in enumerate(grp):
-                call.append((i, pool[k * n:(k + 1) * n]))
-        calls.append(call)
-    return calls
+def _s1(topo, sender, pair):
+    tg = [p for p, o in enumerate(pair) if o["sum"] != sender]
+    engs = _common(topo, sender, [pair[p]["sum"] for p in tg])
+    near = [p for p in tg if pair[p]["die"] == topo.die(sender)]
+    far = [p for p in tg if pair[p]["die"] != topo.die(sender)]
+    if near and far:
+        return [(near[0], engs[0::2]), (far[0], engs[1::2])]
+    return [(tg[0], engs)]
+
+
+def _s2(topo, o, far_o):
+    ef = _bits(topo.mask(o["sum"], far_o["fin"]))
+    out = [(far_o["fin"], ef, "land2")]
+    if o["fin"] != o["sum"]:
+        out.append((o["fin"], [e for e in _bits(topo.mask(o["sum"], o["fin"])) if e not in ef], "landp"))
+    return out
+
+
+def _s3(topo, fin, mine):
+    engs = _common(topo, fin, mine)
+    near = [r for r in mine if topo.die(r) == topo.die(fin)]
+    far = [r for r in mine if topo.die(r) != topo.die(fin)]
+    return [(near, engs[0::2]), (far, engs[1::2])]
 
 
 def _dst(topo, c):
@@ -98,13 +105,9 @@ def rank_program(g, core, T, topo):
     ch = topo.chip(core)
     if ch not in lay:
         return
-    mine, owners = lay[ch]
-    peers = [lay[k] for k in lay if k != ch][0][1]
-    me = [i for i, o in enumerate(owners) if o["core"] == core]
-    me = me[0] if me else None
+    mine, own = lay[ch]
+    far_own = [lay[k] for k in lay if k != ch][0][1]
     is_rank = core in mine
-    if not is_rank and me is None:
-        return
     S = T.sem
     v, sc, sy, te = g.vector, g.scalar, g.sync, g.tensor
     sent = 0
@@ -113,14 +116,8 @@ def rank_program(g, core, T, topo):
         sc.dma_start(T.idx32[0:16, :], T.idx[:, :]).then_inc(S.six, 16)
         sy.dma_start(T.xs[:, :], T.x[:, :]).then_inc(S.sx, 16)
         v.memset(T.onesf[0:16, :], 1.0).then_inc(S.sone, 1)
-        n1 = 1
-        if me is not None:
-            v.memset(T.onesb[:, :], 1.0).then_inc(S.sone, 1)
-            n1 = 2
-        g.wait_ge(S.sone, n1)
+        g.wait_ge(S.sone, 1)
         g.affine_select(T.rep[0:16, :], T.onesf[0:16, :], [[0, 8], [-1, 16]], AluOpType.is_equal, 0.0, 0, 1).then_inc(S.srep, 1)
-        if me is not None:
-            g.affine_select(T.ident[:, :], T.onesb[:, :], [[-1, 128]], AluOpType.is_equal, 0.0, 0, 1).then_inc(S.sid, 1)
         v.wait_ge(S.six, 16)
         v.tensor_copy(T.idxf[0:16, :], T.idx32[0:16, :]).then_inc(S.sf, 1)
         te.wait_ge(S.sf, 1)
@@ -131,112 +128,82 @@ def rank_program(g, core, T, topo):
         for q in (v, sc):
             q.wait_ge(S.soff, 1)
             q.wait_ge(S.sx, 16)
-        h = W // 2
         for c in range(C):
             a = c * W
-            v.tensor_copy(T.gat[:, a:a + h],
-                          T.xs[:, 0:NCOL].indirect(T.offs[:, a // 16:(a + h) // 16])).then_inc(S["gat%d" % c], 1)
-            a += h
-            sc.activation(T.gat[:, a:a + h], T.xs[:, 0:NCOL].indirect(T.offs[:, a // 16:(a + h) // 16]),
+            v.tensor_copy(T.gat[:, a:a + H],
+                          T.xs[:, 0:NCOL].indirect(T.offs[:, a // 16:(a + H) // 16])).then_inc(S["gat%d" % c], 1)
+            a += H
+            sc.activation(T.gat[:, a:a + H], T.xs[:, 0:NCOL].indirect(T.offs[:, a // 16:(a + H) // 16]),
                           ActivationFunctionType.Copy).then_inc(S["gat%d" % c], 1)
         pos = mine.index(core)
-        calls = _s1_calls(topo, core, owners)
         for c in range(C):
             g.wait_ge(S["gat%d" % c], 2)
-            for call in calls:
-                trs = []
-                for i, engs in call:
-                    o = owners[i]
-                    y0 = c * W + o["off"]
-                    l0 = pos * SLOT + c * o["w"]
-                    trs.append(RemoteDMATransfer(dst_ids=[_dst(topo, o["core"])], dma_engine_mask=_mask(engs),
-                                                 remote_sem=S["a1_%d" % c], src=T.gat[:, y0:y0 + o["w"]],
-                                                 dst=T.land1[:, l0:l0 + o["w"]]))
-                    sent += len(engs)
-                g.remote_dma_fused(trs, local_sem=S.sent)
+            pair = own[_kind(c)]
+            trs = []
+            for p, engs in _s1(topo, core, pair):
+                y0 = c * W + p * H
+                l0 = pos * SLOT + (c // 2) * H
+                trs.append(RemoteDMATransfer(dst_ids=[_dst(topo, pair[p]["sum"])], dma_engine_mask=_mask(engs),
+                                             remote_sem=S["a1_%d" % c], src=T.gat[:, y0:y0 + H],
+                                             dst=T.land1[:, l0:l0 + H]))
+                sent += len(engs)
+            g.remote_dma_fused(trs, local_sem=S.sent)
 
-    if me is not None:
-        o = owners[me]
-        w = o["w"]
-        peer = peers[me]["core"]
-        exp1 = 0
-        for r in mine:
-            if r != core:
-                for call in _s1_calls(topo, r, owners):
-                    exp1 += sum(len(engs) for i, engs in call if i == me)
-        exp2 = len(_bits(topo.mask(peer, core)))
+    def pieces(c, p):
+        out = []
+        for s, r in enumerate(mine):
+            if r == core:
+                out.append(T.gat[:, c * W + p * H:c * W + (p + 1) * H])
+            else:
+                out.append(T.land1[:, s * SLOT + (c // 2) * H:s * SLOT + (c // 2 + 1) * H])
+        return out
 
-        def pieces(c, lo, n):
-            out = []
-            for s, r in enumerate(mine):
-                if r == core:
-                    out.append(T.gat[:, c * W + o["off"] + lo:c * W + o["off"] + lo + n])
-                else:
-                    out.append(T.land1[:, s * SLOT + c * w + lo:s * SLOT + c * w + lo + n])
-            return out
-
-        e2 = _bits(topo.mask(core, peer))
-        for c in range(C):
+    for c in range(C):
+        for p, o in enumerate(own[_kind(c)]):
+            if o["sum"] != core:
+                continue
+            exp1 = 0
+            for r in mine:
+                if r != core:
+                    exp1 += sum(len(engs) for q, engs in _s1(topo, r, own[_kind(c)]) if q == p)
             g.wait_ge(S["a1_%d" % c], exp1)
-            g.remote_dma_fused([RemoteDMATransfer(dst_ids=[_dst(topo, peer)], dma_engine_mask=_mask(e2),
-                                                  remote_sem=S["a2_%d" % c], srcs=pieces(c, 0, w),
-                                                  dsts=[T.land2[:, c * w:(c + 1) * w]], alu_op=1)], local_sem=S.sent)
-            sent += len(e2)
-        dests = [r for r in mine if r != core]
-        m3 = topo.mask(core, dests[0])
-        for r in dests:
-            m3 &= topo.mask(core, r)
-        e3 = _bits(m3)
-        for c in range(C):
+            j = (c // 2) * H
+            trs = []
+            for fin, engs, name in _s2(topo, o, far_own[_kind(c)][p]):
+                trs.append(RemoteDMATransfer(dst_ids=[_dst(topo, fin)], dma_engine_mask=_mask(engs),
+                                             remote_sem=S["a2_%d" % c], srcs=pieces(c, p),
+                                             dsts=[T[name][:, j:j + H]], alu_op=1))
+                sent += len(engs)
+            g.remote_dma_fused(trs, local_sem=S.sent)
+
+    for c in range(C):
+        for p, o in enumerate(own[_kind(c)]):
+            if o["fin"] != core:
+                continue
+            exp2 = sum(len(engs) for fin, engs, name in _s2(topo, far_own[_kind(c)][p], o) if fin == core)
+            exp2 += sum(len(engs) for fin, engs, name in _s2(topo, o, far_own[_kind(c)][p]) if fin == core)
             g.wait_ge(S["a2_%d" % c], exp2)
-            y0 = c * W + o["off"]
-            g.remote_dma_fused([RemoteDMATransfer(dst_ids=[_dst(topo, r) for r in dests], dma_engine_mask=_mask(e3),
-                                                  remote_sem=S["a3_%d_%d" % (c, o["part"])],
-                                                  srcs=pieces(c, 0, w) + [T.land2[:, c * w:(c + 1) * w]],
-                                                  dsts=[T.res[:, y0:y0 + w] for r in dests], alu_op=1)],
-                               local_sem=S.sent)
-            sent += len(e3)
-        if is_rank:
-            te.wait_ge(S.sid, 1)
-            for c in range(C):
-                te.wait_ge(S["gat%d" % c], 2)
-                te.wait_ge(S["a1_%d" % c], exp1)
-                for b in range(NB):
-                    p0 = (c * NB + b) * 512
-                    for k, src in enumerate(pieces(c, b * BW, BW)):
-                        te.matmul(T.ps[:, p0:p0 + BW], T.ident[:, :], src, k == 0, False)
-            for c in range(C):
-                te.wait_ge(S["a2_%d" % c], exp2)
-                for b in range(NB):
-                    p0 = (c * NB + b) * 512
-                    te.matmul(T.ps[:, p0:p0 + BW], T.ident[:, :], T.land2[:, c * w + b * BW:c * w + (b + 1) * BW],
-                              False, True).then_inc(S["mm%d" % c], 1)
-            for c in range(C):
-                v.wait_ge(S["mm%d" % c], NB)
-                for b in range(NB):
-                    p0 = (c * NB + b) * 512
-                    y0 = c * W + o["off"] + b * BW
-                    v.tensor_copy(T.res[:, y0:y0 + BW], T.ps[:, p0:p0 + BW]).then_inc(S["own%d" % c], 1)
+            j = (c // 2) * H
+            srcs = (pieces(c, p) if o["sum"] == core else [T.landp[:, j:j + H]]) + [T.land2[:, j:j + H]]
+            y0 = c * W + p * H
+            trs = []
+            for dests, engs in _s3(topo, core, mine):
+                trs.append(RemoteDMATransfer(dst_ids=[_dst(topo, r) for r in dests], dma_engine_mask=_mask(engs),
+                                             remote_sem=S["a3_%d_%d" % (c, p)], srcs=srcs,
+                                             dsts=[T.res[:, y0:y0 + H] for r in dests], alu_op=1))
+                sent += len(engs)
+            g.remote_dma_fused(trs, local_sem=S.sent)
 
     if is_rank:
-        h = W // 2
         for c in range(C):
-            for part, q in enumerate((sy, sc)):
-                exp3 = 0
-                for i, o in enumerate(owners):
-                    if o["part"] == part and o["core"] != core:
-                        ds = [r for r in mine if r != o["core"]]
-                        m = topo.mask(o["core"], ds[0])
-                        for r in ds:
-                            m &= topo.mask(o["core"], r)
-                        exp3 += len(_bits(m))
-                if exp3:
-                    q.wait_ge(S["a3_%d_%d" % (c, part)], exp3)
-                if me is not None and owners[me]["part"] == part:
-                    q.wait_ge(S["own%d" % c], NB)
-                a = c * W + part * h
-                q.dma_start(T.y[:, a:a + h], T.res[:, a:a + h]).then_inc(S["st%d" % part], 16)
+            for p, q in enumerate((sy, sc)):
+                fin = own[_kind(c)][p]["fin"]
+                exp3 = sum(len(engs) for dests, engs in _s3(topo, fin, mine) if core in dests)
+                q.wait_ge(S["a3_%d_%d" % (c, p)], exp3)
+                a = c * W + p * H
+                q.dma_start(T.y[:, a:a + H], T.res[:, a:a + H]).then_inc(S["st%d" % p], 16)
         sy.wait_ge(S.st0, 16 * C)
         sc.wait_ge(S.st1, 16 * C)
 
-    g.wait_ge(S.sent, sent)
+    if sent:
+        g.wait_ge(S.sent, sent)

@@ -7,7 +7,7 @@ M = 2048
 C = 4
 W = M // C
 H = W // 2
-SLOT = (C // 2) * H
+K = C // 2
 
 SCRATCH = {
     "xs": ("sbuf", [128, NCOL], "bfloat16"),
@@ -17,14 +17,15 @@ SCRATCH = {
     "rep": ("sbuf", [128, 128], "float32"),
     "offs": ("sbuf", [128, 128], "uint16"),
     "gat": ("sbuf", [128, M], "bfloat16"),
-    "land1": ("sbuf", [128, 4 * SLOT], "bfloat16"),
-    "landp": ("sbuf", [128, SLOT], "bfloat16"),
-    "land2": ("sbuf", [128, SLOT], "bfloat16"),
-    "res": ("sbuf", [128, M], "bfloat16"),
+    "dl1": ("dram", [4 * K, 128, H], "bfloat16"),
+    "dlp": ("dram", [K, 128, H], "bfloat16"),
+    "dl2": ("dram", [K, 128, H], "bfloat16"),
+    "dres": ("dram", [2 * C, 128, H], "bfloat16"),
     "psoff": ("psum", [128, 128], "float32"),
 }
 SEMAPHORES = (["six", "sx", "sone", "srep", "sf", "spo", "soff", "sent", "st0", "st1"]
               + ["gat%d" % c for c in range(C)] + ["a1_%d" % c for c in range(C)] + ["a2_%d" % c for c in range(C)]
+              + ["cp%d" % c for c in range(C)]
               + ["a3_%d_%d" % (c, p) for c in range(C) for p in range(2)])
 
 
@@ -82,9 +83,9 @@ def _s1(topo, sender, pair):
 
 def _s2(topo, o, far_o):
     ef = _bits(topo.mask(o["sum"], far_o["fin"]))
-    out = [(far_o["fin"], ef, "land2")]
+    out = [(far_o["fin"], ef, "dl2")]
     if o["fin"] != o["sum"]:
-        out.append((o["fin"], [e for e in _bits(topo.mask(o["sum"], o["fin"])) if e not in ef], "landp"))
+        out.append((o["fin"], [e for e in _bits(topo.mask(o["sum"], o["fin"])) if e not in ef], "dlp"))
     return out
 
 
@@ -142,21 +143,19 @@ def rank_program(g, core, T, topo):
             trs = []
             for p, engs in _s1(topo, core, pair):
                 y0 = c * W + p * H
-                l0 = pos * SLOT + (c // 2) * H
                 trs.append(RemoteDMATransfer(dst_ids=[_dst(topo, pair[p]["sum"])], dma_engine_mask=_mask(engs),
                                              remote_sem=S["a1_%d" % c], src=T.gat[:, y0:y0 + H],
-                                             dst=T.land1[:, l0:l0 + H]))
+                                             dst=T.dl1[pos * K + c // 2]))
                 sent += len(engs)
             g.remote_dma_fused(trs, local_sem=S.sent)
+            for p, o in enumerate(pair):
+                if o["sum"] == core:
+                    y0 = c * W + p * H
+                    sy.wait_ge(S["gat%d" % c], 2)
+                    sy.dma_start(T.dl1[pos * K + c // 2], T.gat[:, y0:y0 + H]).then_inc(S["cp%d" % c], 16)
 
-    def pieces(c, p):
-        out = []
-        for s, r in enumerate(mine):
-            if r == core:
-                out.append(T.gat[:, c * W + p * H:c * W + (p + 1) * H])
-            else:
-                out.append(T.land1[:, s * SLOT + (c // 2) * H:s * SLOT + (c // 2 + 1) * H])
-        return out
+    def pieces(c):
+        return [T.dl1[s * K + c // 2] for s in range(len(mine))]
 
     for c in range(C):
         for p, o in enumerate(own[_kind(c)]):
@@ -166,13 +165,14 @@ def rank_program(g, core, T, topo):
             for r in mine:
                 if r != core:
                     exp1 += sum(len(engs) for q, engs in _s1(topo, r, own[_kind(c)]) if q == p)
+            if is_rank:
+                g.wait_ge(S["cp%d" % c], 16)
             g.wait_ge(S["a1_%d" % c], exp1)
-            j = (c // 2) * H
             trs = []
             for fin, engs, name in _s2(topo, o, far_own[_kind(c)][p]):
                 trs.append(RemoteDMATransfer(dst_ids=[_dst(topo, fin)], dma_engine_mask=_mask(engs),
-                                             remote_sem=S["a2_%d" % c], srcs=pieces(c, p),
-                                             dsts=[T[name][:, j:j + H]], alu_op=1))
+                                             remote_sem=S["a2_%d" % c], srcs=pieces(c),
+                                             dsts=[T[name][c // 2]], alu_op=1))
                 sent += len(engs)
             g.remote_dma_fused(trs, local_sem=S.sent)
 
@@ -183,14 +183,12 @@ def rank_program(g, core, T, topo):
             exp2 = sum(len(engs) for fin, engs, name in _s2(topo, far_own[_kind(c)][p], o) if fin == core)
             exp2 += sum(len(engs) for fin, engs, name in _s2(topo, o, far_own[_kind(c)][p]) if fin == core)
             g.wait_ge(S["a2_%d" % c], exp2)
-            j = (c // 2) * H
-            srcs = (pieces(c, p) if o["sum"] == core else [T.landp[:, j:j + H]]) + [T.land2[:, j:j + H]]
-            y0 = c * W + p * H
+            srcs = (pieces(c) if o["sum"] == core else [T.dlp[c // 2]]) + [T.dl2[c // 2]]
             trs = []
             for dests, engs in _s3(topo, core, mine):
                 trs.append(RemoteDMATransfer(dst_ids=[_dst(topo, r) for r in dests], dma_engine_mask=_mask(engs),
                                              remote_sem=S["a3_%d_%d" % (c, p)], srcs=srcs,
-                                             dsts=[T.res[:, y0:y0 + H] for r in dests], alu_op=1))
+                                             dsts=[T.dres[2 * c + p] for r in dests], alu_op=1))
                 sent += len(engs)
             g.remote_dma_fused(trs, local_sem=S.sent)
 
@@ -201,7 +199,7 @@ def rank_program(g, core, T, topo):
                 exp3 = sum(len(engs) for dests, engs in _s3(topo, fin, mine) if core in dests)
                 q.wait_ge(S["a3_%d_%d" % (c, p)], exp3)
                 a = c * W + p * H
-                q.dma_start(T.y[:, a:a + H], T.res[:, a:a + H]).then_inc(S["st%d" % p], 16)
+                q.dma_start(T.y[:, a:a + H], T.dres[2 * c + p]).then_inc(S["st%d" % p], 16)
         sy.wait_ge(S.st0, 16 * C)
         sc.wait_ge(S.st1, 16 * C)
 

@@ -65,8 +65,8 @@ def _layout(T, topo):
             rk = [c for c in port if c in mine][0]
             hp = [c for c in port if c not in mine][0]
             hn = [c for c in on_die if c not in mine and c not in port][0]
-            own[0].append({"sum": rk, "fin": hn, "die": d})
-            own[1].append({"sum": hp, "fin": hp, "die": d})
+            own[0].append({"sum": rk, "fin": hp, "die": d})
+            own[1].append({"sum": hp, "fin": hn, "die": d})
         lay[ch] = (mine, own)
     return lay
 

from concourse.bass import DstId, RemoteDMATransfer
from concourse.mybir import AluOpType, ActivationFunctionType

SIM_CORES = 64
NCOL = 8192
M = 2048
C = 4
W = M // C
H = W // 2
K = C // 2

SCRATCH = {
    "xs": ("sbuf", [128, NCOL], "bfloat16"),
    "idx32": ("sbuf", [128, 128], "int32"),
    "idxf": ("sbuf", [128, 128], "float32"),
    "onesf": ("sbuf", [128, 128], "float32"),
    "rep": ("sbuf", [128, 128], "float32"),
    "offs": ("sbuf", [128, 128], "uint16"),
    "gat": ("sbuf", [128, M], "bfloat16"),
    "dl1": ("dram", [4 * K, 128, H], "bfloat16"),
    "dlp": ("dram", [K, 128, H], "bfloat16"),
    "dl2": ("dram", [K, 128, H], "bfloat16"),
    "dres": ("dram", [2 * C, 128, H], "bfloat16"),
    "psoff": ("psum", [128, 128], "float32"),
}
SEMAPHORES = (["six", "sx", "sone", "srep", "sf", "spo", "soff", "sent", "st0", "st1"]
              + ["gat%d" % c for c in range(C)] + ["a1_%d" % c for c in range(C)] + ["a2_%d" % c for c in range(C)]
              + ["cp%d" % c for c in range(C)]
              + ["a3_%d_%d" % (c, p) for c in range(C) for p in range(2)])


def _kind(c):
    return (c + 1) % 2


def _bits(mask):
    return [e for e in range(mask.bit_length()) if (mask >> e) & 1]


def _mask(engs):
    m = 0
    for e in engs:
        m |= 1 << e
    return m


def _common(topo, src, dsts):
    m = topo.mask(src, dsts[0])
    for d in dsts:
        m &= topo.mask(src, d)
    return _bits(m)


def _layout(T, topo):
    ranks = list(T.cores)
    lay = {}
    for ch in sorted({topo.chip(c) for c in ranks}):
        mine = [c for c in ranks if topo.chip(c) == ch]
        far = [c for c in ranks if topo.chip(c) != ch]
        here = [c for c in range(SIM_CORES) if topo.chip(c) == ch]
        own = [[], []]
        for d in sorted({topo.die(c) for c in mine}):
            on_die = [c for c in here if topo.die(c) == d]
            port = [c for c in on_die if all(topo.may_write(c, f) for f in far)]
            rk = [c for c in port if c in mine][0]
            hp = [c for c in port if c not in mine][0]
            hn = [c for c in on_die if c not in mine and c not in port][0]
            own[0].append({"sum": rk, "fin": hp, "die": d})
            own[1].append({"sum": hp, "fin": hn, "die": d})
        lay[ch] = (mine, own)
    return lay


def _s1(topo, sender, pair):
    tg = [p for p, o in enumerate(pair) if o["sum"] != sender]
    engs = _common(topo, sender, [pair[p]["sum"] for p in tg])
    near = [p for p in tg if pair[p]["die"] == topo.die(sender)]
    far = [p for p in tg if pair[p]["die"] != topo.die(sender)]
    if near and far:
        return [(near[0], engs[0::2]), (far[0], engs[1::2])]
    return [(tg[0], engs)]


def _s2(topo, o, far_o):
    ef = _bits(topo.mask(o["sum"], far_o["fin"]))
    out = [(far_o["fin"], ef, "dl2")]
    if o["fin"] != o["sum"]:
        out.append((o["fin"], [e for e in _bits(topo.mask(o["sum"], o["fin"])) if e not in ef], "dlp"))
    return out


def _s3(topo, fin, mine):
    engs = _common(topo, fin, mine)
    near = [r for r in mine if topo.die(r) == topo.die(fin)]
    far = [r for r in mine if topo.die(r) != topo.die(fin)]
    return [(near, engs[0::2]), (far, engs[1::2])]


def _dst(topo, c):
    rid, pid, _ = topo.addr(c)
    return DstId(rid=rid, pnc=pid)


def rank_program(g, core, T, topo):
    lay = _layout(T, topo)
    ch = topo.chip(core)
    if ch not in lay:
        return
    mine, own = lay[ch]
    far_own = [lay[k] for k in lay if k != ch][0][1]
    is_rank = core in mine
    S = T.sem
    v, sc, sy, te = g.vector, g.scalar, g.sync, g.tensor
    sent = 0

    if is_rank:
        sc.dma_start(T.idx32[0:16, :], T.idx[:, :]).then_inc(S.six, 16)
        sy.dma_start(T.xs[:, :], T.x[:, :]).then_inc(S.sx, 16)
        v.memset(T.onesf[0:16, :], 1.0).then_inc(S.sone, 1)
        g.wait_ge(S.sone, 1)
        g.affine_select(T.rep[0:16, :], T.onesf[0:16, :], [[0, 8], [-1, 16]], AluOpType.is_equal, 0.0, 0, 1).then_inc(S.srep, 1)
        v.wait_ge(S.six, 16)
        v.tensor_copy(T.idxf[0:16, :], T.idx32[0:16, :]).then_inc(S.sf, 1)
        te.wait_ge(S.sf, 1)
        te.wait_ge(S.srep, 1)
        te.matmul(T.psoff[:, :], T.rep[0:16, :], T.idxf[0:16, :], True, True).then_inc(S.spo, 1)
        v.wait_ge(S.spo, 1)
        v.tensor_copy(T.offs[:, :], T.psoff[:, :]).then_inc(S.soff, 1)
        for q in (v, sc):
            q.wait_ge(S.soff, 1)
            q.wait_ge(S.sx, 16)
        for c in range(C):
            a = c * W
            v.tensor_copy(T.gat[:, a:a + H],
                          T.xs[:, 0:NCOL].indirect(T.offs[:, a // 16:(a + H) // 16])).then_inc(S["gat%d" % c], 1)
            a += H
            sc.activation(T.gat[:, a:a + H], T.xs[:, 0:NCOL].indirect(T.offs[:, a // 16:(a + H) // 16]),
                          ActivationFunctionType.Copy).then_inc(S["gat%d" % c], 1)
        pos = mine.index(core)
        for c in range(C):
            g.wait_ge(S["gat%d" % c], 2)
            pair = own[_kind(c)]
            trs = []
            for p, engs in _s1(topo, core, pair):
                y0 = c * W + p * H
                trs.append(RemoteDMATransfer(dst_ids=[_dst(topo, pair[p]["sum"])], dma_engine_mask=_mask(engs),
                                             remote_sem=S["a1_%d" % c], src=T.gat[:, y0:y0 + H],
                                             dst=T.dl1[pos * K + c // 2]))
                sent += len(engs)
            g.remote_dma_fused(trs, local_sem=S.sent)
            for p, o in enumerate(pair):
                if o["sum"] == core:
                    y0 = c * W + p * H
                    sy.wait_ge(S["gat%d" % c], 2)
                    sy.dma_start(T.dl1[pos * K + c // 2], T.gat[:, y0:y0 + H]).then_inc(S["cp%d" % c], 16)

    def pieces(c):
        return [T.dl1[s * K + c // 2] for s in range(len(mine))]

    for c in range(C):
        for p, o in enumerate(own[_kind(c)]):
            if o["sum"] != core:
                continue
            exp1 = 0
            for r in mine:
                if r != core:
                    exp1 += sum(len(engs) for q, engs in _s1(topo, r, own[_kind(c)]) if q == p)
            if is_rank:
                g.wait_ge(S["cp%d" % c], 16)
            g.wait_ge(S["a1_%d" % c], exp1)
            trs = []
            for fin, engs, name in _s2(topo, o, far_own[_kind(c)][p]):
                trs.append(RemoteDMATransfer(dst_ids=[_dst(topo, fin)], dma_engine_mask=_mask(engs),
                                             remote_sem=S["a2_%d" % c], srcs=pieces(c),
                                             dsts=[T[name][c // 2]], alu_op=1))
                sent += len(engs)
            g.remote_dma_fused(trs, local_sem=S.sent)

    for c in range(C):
        for p, o in enumerate(own[_kind(c)]):
            if o["fin"] != core:
                continue
            exp2 = sum(len(engs) for fin, engs, name in _s2(topo, far_own[_kind(c)][p], o) if fin == core)
            exp2 += sum(len(engs) for fin, engs, name in _s2(topo, o, far_own[_kind(c)][p]) if fin == core)
            g.wait_ge(S["a2_%d" % c], exp2)
            srcs = (pieces(c) if o["sum"] == core else [T.dlp[c // 2]]) + [T.dl2[c // 2]]
            trs = []
            for dests, engs in _s3(topo, core, mine):
                trs.append(RemoteDMATransfer(dst_ids=[_dst(topo, r) for r in dests], dma_engine_mask=_mask(engs),
                                             remote_sem=S["a3_%d_%d" % (c, p)], srcs=srcs,
                                             dsts=[T.dres[2 * c + p] for r in dests], alu_op=1))
                sent += len(engs)
            g.remote_dma_fused(trs, local_sem=S.sent)

    if is_rank:
        for c in range(C):
            for p, q in enumerate((sy, sc)):
                fin = own[_kind(c)][p]["fin"]
                exp3 = sum(len(engs) for dests, engs in _s3(topo, fin, mine) if core in dests)
                q.wait_ge(S["a3_%d_%d" % (c, p)], exp3)
                a = c * W + p * H
                q.dma_start(T.y[:, a:a + H], T.dres[2 * c + p]).then_inc(S["st%d" % p], 16)
        sy.wait_ge(S.st0, 16 * C)
        sc.wait_ge(S.st1, 16 * C)

    if sent:
        g.wait_ge(S.sent, sent)
